import numpy as np
import ml_dtypes


def mxq(x, axis, fmt="e4m3"):
    dtype, down = {"e4m3": (ml_dtypes.float8_e4m3fn, 7), "e5m2": (ml_dtypes.float8_e5m2, 14)}[fmt]
    v = np.moveaxis(np.asarray(x, np.float32).astype(ml_dtypes.bfloat16).astype(np.float64), axis, -1)
    blocks = v.reshape(v.shape[:-1] + (-1, 32))
    amax = np.abs(blocks).max(-1, keepdims=True)
    byte = np.maximum(np.where(amax > 0, np.frexp(amax)[1] - 1 + 127, 0) - down, 1)
    scale = np.exp2(byte - 127.0)
    codes = (blocks / scale).astype(np.float32).astype(dtype).astype(np.float64)
    return np.moveaxis((codes * scale).reshape(v.shape), -1, axis)


WIDE = False


def mx_kscale(k):
    if not WIDE:
        return np.ones(k)
    levels = np.array([10, -10, 5, -5, 0])
    if k % 512:
        return np.exp2(np.random.permutation(np.resize(levels, k // 32))).repeat(32)
    a = np.empty((k // 512, 16))
    for p in range(k // 512):
        a[p, :8] = np.random.permutation(np.resize(levels, 8))
        for g in range(8):
            far = levels[np.abs(levels - a[p, g]) >= 10]
            a[p, g + 8] = far[np.random.randint(len(far))]
    return np.exp2(a.ravel()).repeat(32)


def f64(x):
    return np.asarray(x).astype(np.float64)


def striped(idx):
    return np.tile(np.asarray(idx).reshape(-1, 16).T, (8, 1)).astype(np.uint16)


def unstriped(offs):
    return offs[:16].T.reshape(-1).astype(np.int64)


E2M1 = np.array([0.0, 0.5, 1.0, 1.5, 2.0, 3.0, 4.0, 6.0, -0.0, -0.5, -1.0, -1.5, -2.0, -3.0, -4.0, -6.0])


def pack_weight(w, fmt):
    k, n = w.shape
    w = f64(np.asarray(w, np.float32).astype(ml_dtypes.bfloat16)).reshape(k // 32, 32, n)
    amax = np.abs(w).max(1)
    if fmt == "e4m3":
        byte = np.frexp(amax)[1] - 1 + 127 - 7
    else:
        mant, ex = np.frexp(amax / 6.0)
        byte = np.where(mant > 0.5, ex, ex - 1) + 127
    byte = np.clip(np.where(amax > 0, byte, 1), 1, 254)
    scaled = (w * np.exp2(127.0 - byte)[:, None, :]).reshape(k, n).astype(np.float32)
    by_word = np.ascontiguousarray(scaled.reshape(k // 512, 128, 4, n).transpose(0, 1, 3, 2))
    if fmt == "e4m3":
        words = by_word.astype(ml_dtypes.float8_e4m3fn).view(np.uint8)
    else:
        c = by_word.astype(ml_dtypes.float4_e2m1fn).view(np.uint8) & 0xF
        words = (c[..., 0::2] | (c[..., 1::2] << 4)).reshape(k // 512, 128, 2 * n)
    return np.ascontiguousarray(words), np.ascontiguousarray(byte.astype(np.uint8).reshape(k // 512, 16, n))


def unpack_weight(words, scales, fmt):
    g, _, n = scales.shape
    words = np.ascontiguousarray(words).reshape(g, 128, n, -1)
    if fmt == "e4m3":
        vals = words.view(ml_dtypes.float8_e4m3fn).astype(np.float64)
    else:
        nib = np.empty((g, 128, n, 4), np.uint8)
        nib[..., 0::2] = words & 0xF
        nib[..., 1::2] = words >> 4
        vals = E2M1[nib]
    vals = vals * np.repeat(np.exp2(scales.astype(np.float64) - 127.0), 8, axis=1)[..., None]
    return vals.transpose(0, 1, 3, 2).reshape(g * 512, n)


def bf(x):
    return np.asarray(x, np.float32).astype(ml_dtypes.bfloat16)


def planes(Y):
    r, m = Y.shape
    b = f64(bf(Y)).reshape(r // 32, 32, m)
    amax = np.abs(b).max(1)
    byte = np.clip(np.where(amax > 0, np.frexp(amax)[1] - 1 + 127 - 7, 1), 1, 254)
    codes = (b * np.exp2(127.0 - byte)[:, None, :]).reshape(r, m).astype(np.float32).astype(ml_dtypes.float8_e4m3fn).view(np.uint8)
    words = codes.reshape(r // 512, 128, 4, m).transpose(0, 1, 3, 2)
    return np.ascontiguousarray(words), np.ascontiguousarray(byte.astype(np.uint8).reshape(r // 512, 16, m))


D, R, T, I, Q = 512, 512, 2048, 512, 512


def setup_inputs():
    n = np.random.standard_normal
    idx = np.random.permutation(T)[:I]
    fd = mx_kscale(D)
    fr = mx_kscale(R)
    latp = pack_weight(n((R, T)) / fr[:, None], "e2m1")
    return {
        "query": (n((D, Q)) * 0.8 / np.sqrt(D) * fd[:, None]).astype(np.float32),
        "up": (n((R, D)) * 0.5 / np.sqrt(R) * fr[:, None] / fd).astype(np.float32),
        "lat_words": latp[0],
        "lat_scales": latp[1],
        "keys": (n((D, T)) / fd[:, None]).astype(np.float32),
        "offs": striped(idx),
    }


def reference(query, up, lat_words, lat_scales, keys, offs):
    idx = unstriped(offs)
    latu = unpack_weight(lat_words, lat_scales, "e2m1")
    upq = mxq(f64(up), 0, "e4m3")
    latidxg = latu[:, idx]
    z = upq.T @ latidxg
    km = z + f64(keys)[:, idx]
    queryq = mxq(f64(query), 0, "e4m3")
    kmq = mxq(km, 0, "e4m3")
    a = queryq.T @ kmq
    p = np.exp(a - np.max(a, axis=1, keepdims=True))
    y = p / np.sum(p, axis=1, keepdims=True) * 512.0
    words, scales = planes(y)
    return y, words, scales

@@ -1,0 +1,155 @@
+from contextlib import ExitStack
+
+import concourse.mybir as mybir
+
+D, R, T, I, Q = 512, 512, 2048, 512, 512
+FLOPS = 2 * R * D * I + 2 * D * Q * I
+
+F32 = mybir.dt.float32
+BF16 = mybir.dt.bfloat16
+I32 = mybir.dt.int32
+U32 = mybir.dt.uint32
+U16 = mybir.dt.uint16
+U8 = mybir.dt.uint8
+FP8X4 = mybir.dt.float8_e4m3fn_x4
+FP4X4 = mybir.dt.float4_e2m1fn_x4
+ALU = mybir.AluOpType
+ACT = mybir.ActivationFunctionType
+AX = mybir.AxisListType
+
+P = 128
+PACK = 4
+
+
+def tile_attend_lowrankdelta_pl_kernel(tc, query, up, lat_words, lat_scales, keys, offs, out_0, out_1, out_2):
+    nc = tc.nc
+    with ExitStack() as ctx:
+        sb = ctx.enter_context(tc.tile_pool(name="sb", bufs=1))
+        ps = ctx.enter_context(tc.psum_pool(name="ps", bufs=1))
+
+        offsets = sb.tile([P, I // 16], U16, name="offsets")
+        nc.sync.dma_start(offsets[:], offs)
+
+        lat_s = sb.tile([P, T], U8, name="lat_s", align_bytes=64)
+        nc.vector.memset(lat_s[:].bitcast(I32), 0)
+        warm_in = sb.tile([P, 1], F32, name="warm_in")
+        warm_out = sb.tile([P, 1], F32, name="warm_out")
+        nc.vector.memset(warm_in[:], 0.0)
+        for g in range(4):
+            nc.scalar.dma_start(lat_s[32 * g : 32 * g + 4, :].bitcast(I32), lat_scales[0, 4 * g : 4 * g + 4, :].bitcast(I32))
+        nc.scalar.activation(warm_out[:], warm_in[:], ACT.Exp)
+
+        lat_w = sb.tile([P, T], U16, name="lat_w", align_bytes=64)
+        nc.sync.dma_start(lat_w[:].bitcast(I32), lat_words[0].bitcast(I32))
+
+        up_rows = up.rearrange("(p j) c -> p j c", j=PACK)
+        up_raw = []
+        for h in range(2):
+            raw = sb.tile([P, PACK, D // 2], F32, name=f"up_raw{h}")
+            nc.sync.dma_start(raw[:], up_rows[:, :, h * 256 : (h + 1) * 256])
+            up_raw.append(raw)
+
+        key_rows = keys.rearrange("(p j) c -> p j c", j=PACK)
+        key_pl = []
+        for j in range(PACK):
+            pl = sb.tile([P, T], F32, name=f"keys{j}")
+            nc.sync.dma_start(pl[:], key_rows[:, j, :])
+            key_pl.append(pl)
+
+        q_rows = query.rearrange("(p j) c -> p j c", j=PACK)
+        q_raw = []
+        for h in range(4):
+            raw = sb.tile([P, PACK, Q // 4], F32, name=f"q_raw{h}")
+            nc.sync.dma_start(raw[:], q_rows[:, :, h * 128 : (h + 1) * 128])
+            q_raw.append(raw)
+
+        g_s = sb.tile([P, I], U8, name="g_s", align_bytes=64)
+        nc.vector.tensor_copy(g_s[:], lat_s[:].indirect(offsets[:]))
+        g_w = sb.tile([P, I], U16, name="g_w", align_bytes=64)
+        nc.vector.tensor_copy(g_w[:], lat_w[:].indirect(offsets[:]))
+
+        up_bf = sb.tile([P, PACK, P, PACK], BF16, name="up_bf", align_bytes=64)
+        for h in range(2):
+            dst = up_bf[:, :, h * 64 : (h + 1) * 64, :].rearrange("p t m j -> p m j t")
+            src = up_raw[h][:].rearrange("p j (m t) -> p m j t", t=PACK)
+            if h == 0:
+                nc.scalar.copy(dst, src)
+            else:
+                nc.vector.tensor_copy(dst, src)
+        up_c = sb.tile([P, D], U32, name="up_c", align_bytes=64)
+        up_s = sb.tile([P, D], U8, name="up_s", align_bytes=64)
+        nc.vector.quantize_mx(out=up_c[:].bitcast(FP8X4), scales=up_s[:], in_=up_bf[:].rearrange("p t m j -> p (t m j)"))
+
+        km_bf = sb.tile([P, I, PACK], BF16, name="km_bf", align_bytes=64)
+        km = [sb.tile([P, 2, I], F32, name=f"km{h}") for h in range(2)]
+        for t in range(PACK):
+            z = ps.tile([P, I], F32, name=f"z{t}")
+            cols = slice(t * P, (t + 1) * P)
+            nc.tensor.matmul_mx(out=z[:], lhsT=up_c[:, cols].bitcast(FP8X4), lhsT_scale=up_s[:, cols],
+                                rhs=g_w[:].bitcast(FP4X4), rhs_scale=g_s[:], start=True, stop=True)
+            z_sb = sb.tile([P, I], F32, name=f"z_sb{t}")
+            nc.scalar.copy(z_sb[:], z[:])
+            nc.vector.tensor_tensor(km[t // 2][:, t % 2, :], key_pl[t][:].indirect(offsets[:]), z_sb[:], ALU.add)
+            if t % 2 == 1:
+                h = t // 2
+                dst = km_bf[:, :, 2 * h : 2 * h + 2].rearrange("p (c i) t -> p c t i", i=4)
+                src = km[h][:].rearrange("p t (c i) -> p c t i", i=4)
+                if h == 0:
+                    nc.scalar.copy(dst, src)
+                else:
+                    nc.vector.tensor_copy(dst, src)
+        km_c = sb.tile([P, I], U32, name="km_c", align_bytes=64)
+        km_s = sb.tile([P, I], U8, name="km_s", align_bytes=64)
+        nc.vector.quantize_mx(out=km_c[:].bitcast(FP8X4), scales=km_s[:], in_=km_bf[:].rearrange("p i t -> p (i t)"))
+
+        q_bf = sb.tile([P, PACK, P, PACK], BF16, name="q_bf", align_bytes=64)
+        for h in range(4):
+            dst = q_bf[:, :, h * 32 : (h + 1) * 32, :].rearrange("p t m j -> p m j t")
+            src = q_raw[h][:].rearrange("p j (m t) -> p m j t", t=PACK)
+            nc.scalar.copy(dst, src)
+
+        y = sb.tile([P, PACK, I], F32, name="y")
+        out_rows = out_0.rearrange("(p t) i -> p t i", t=PACK)
+        scores = []
+        for t in range(PACK):
+            q_c = sb.tile([P, P], U32, name=f"q_c{t}", align_bytes=64)
+            q_s = sb.tile([P, P], U8, name=f"q_s{t}", align_bytes=64)
+            nc.vector.quantize_mx(out=q_c[:].bitcast(FP8X4), scales=q_s[:], in_=q_bf[:, t, :, :].rearrange("p m j -> p (m j)"))
+            a = ps.tile([P, I], F32, name=f"a{t}")
+            nc.tensor.matmul_mx(out=a[:], lhsT=q_c[:].bitcast(FP8X4), lhsT_scale=q_s[:],
+                                rhs=km_c[:].bitcast(FP8X4), rhs_scale=km_s[:], start=True, stop=True)
+            scores.append(a)
+        probs = []
+        for t in range(PACK):
+            nmax = sb.tile([P, 1], F32, name=f"nmax{t}")
+            nc.vector.tensor_reduce(nmax[:], scores[t][:], AX.X, ALU.max, negate=True)
+            e = sb.tile([P, I], F32, name=f"e{t}")
+            s = sb.tile([P, 1], F32, name=f"s{t}")
+            nc.scalar.activation(e[:], scores[t][:], ACT.Exp, bias=nmax[:], scale=1.0, accum_out=s[:])
+            probs.append((e, s))
+        for t in range(PACK):
+            e, s = probs[t]
+            r = sb.tile([P, 1], F32, name=f"r{t}")
+            nc.vector.reciprocal(r[:], s[:])
+            nc.vector.tensor_scalar(y[:, t, :], e[:], r[:], 512.0, ALU.mult, ALU.mult)
+            nc.sync.dma_start(out_rows[:, t, :], y[:, t, :])
+
+        y_bf = sb.tile([P, I, PACK], BF16, name="y_bf", align_bytes=64)
+        for lo, hi, eng in ((0, 256, 0), (384, 512, 1), (256, 384, 0)):
+            dst = y_bf[:, lo:hi, :].rearrange("p (c i) t -> p c t i", i=4)
+            src = y[:, :, lo:hi].rearrange("p t (c i) -> p c t i", i=4)
+            if eng:
+                nc.scalar.copy(dst, src)
+            else:
+                nc.vector.tensor_copy(dst, src)
+        y_c = sb.tile([P, I], U32, name="y_c", align_bytes=64)
+        y_s = sb.tile([P, I], U8, name="y_s", align_bytes=64)
+        words = out_1[0].rearrange("p c t -> p (c t)").bitcast(I32)
+        for h in range(2):
+            cols = slice(h * 256, (h + 1) * 256)
+            nc.vector.quantize_mx(out=y_c[:, cols].bitcast(FP8X4), scales=y_s[:, cols],
+                                  in_=y_bf[:, cols, :].rearrange("p i t -> p (i t)"))
+            nc.sync.dma_start(words[:, cols], y_c[:, cols].bitcast(I32))
+        for g in range(4):
+            eng = nc.scalar if g % 2 else nc.sync
+            eng.dma_start(out_2[0, 4 * g : 4 * g + 4, :].bitcast(I32), y_s[32 * g : 32 * g + 4, :].bitcast(I32))

@@ -43,11 +43,9 @@ def tile_attend_lowrankdelta_pl_kernel(tc, query, up, lat_words, lat_scales, key
         nc.sync.dma_start(lat_w[:].bitcast(I32), lat_words[0].bitcast(I32))
 
         up_rows = up.rearrange("(p j) c -> p j c", j=PACK)
-        up_raw = []
+        up_raw = sb.tile([P, PACK, D], F32, name="up_raw")
         for h in range(2):
-            raw = sb.tile([P, PACK, D // 2], F32, name=f"up_raw{h}")
-            nc.sync.dma_start(raw[:], up_rows[:, :, h * 256 : (h + 1) * 256])
-            up_raw.append(raw)
+            nc.sync.dma_start(up_raw[:, 2 * h : 2 * h + 2, :], up_rows[:, 2 * h : 2 * h + 2, :])
 
         key_rows = keys.rearrange("(p j) c -> p j c", j=PACK)
         key_pl = []
@@ -57,11 +55,8 @@ def tile_attend_lowrankdelta_pl_kernel(tc, query, up, lat_words, lat_scales, key
             key_pl.append(pl)
 
         q_rows = query.rearrange("(p j) c -> p j c", j=PACK)
-        q_raw = []
-        for h in range(4):
-            raw = sb.tile([P, PACK, Q // 4], F32, name=f"q_raw{h}")
-            nc.sync.dma_start(raw[:], q_rows[:, :, h * 128 : (h + 1) * 128])
-            q_raw.append(raw)
+        q_raw = sb.tile([P, PACK, Q], F32, name="q_raw")
+        nc.sync.dma_start(q_raw[:], q_rows)
 
         g_s = sb.tile([P, I], U8, name="g_s", align_bytes=64)
         nc.vector.tensor_copy(g_s[:], lat_s[:].indirect(offsets[:]))
@@ -71,7 +66,7 @@ def tile_attend_lowrankdelta_pl_kernel(tc, query, up, lat_words, lat_scales, key
         up_bf = sb.tile([P, PACK, P, PACK], BF16, name="up_bf", align_bytes=64)
         for h in range(2):
             dst = up_bf[:, :, h * 64 : (h + 1) * 64, :].rearrange("p t m j -> p m j t")
-            src = up_raw[h][:].rearrange("p j (m t) -> p m j t", t=PACK)
+            src = up_raw[:, :, h * 256 : (h + 1) * 256].rearrange("p j (m t) -> p m j t", t=PACK)
             if h == 0:
                 nc.scalar.copy(dst, src)
             else:
@@ -89,24 +84,36 @@ def tile_attend_lowrankdelta_pl_kernel(tc, query, up, lat_words, lat_scales, key
                                 rhs=g_w[:].bitcast(FP4X4), rhs_scale=g_s[:], start=True, stop=True)
             z_sb = sb.tile([P, I], F32, name=f"z_sb{t}")
             nc.scalar.copy(z_sb[:], z[:])
-            nc.vector.tensor_tensor(km[t // 2][:, t % 2, :], key_pl[t][:].indirect(offsets[:]), z_sb[:], ALU.add)
-            if t % 2 == 1:
-                h = t // 2
-                dst = km_bf[:, :, 2 * h : 2 * h + 2].rearrange("p (c i) t -> p c t i", i=4)
-                src = km[h][:].rearrange("p t (c i) -> p c t i", i=4)
-                if h == 0:
-                    nc.scalar.copy(dst, src)
-                else:
-                    nc.vector.tensor_copy(dst, src)
+            if t < PACK - 1:
+                nc.vector.tensor_tensor(km[t // 2][:, t % 2, :], key_pl[t][:].indirect(offsets[:]), z_sb[:], ALU.add)
+            else:
+                for u in range(2):
+                    nc.vector.tensor_tensor(km[1][:, 1, u * 256 : (u + 1) * 256], key_pl[t][:].indirect(offsets[:, u * 16 : (u + 1) * 16]),
+                                            z_sb[:, u * 256 : (u + 1) * 256], ALU.add)
+            if t == 1:
+                nc.scalar.copy(km_bf[:, :, 0:2].rearrange("p (c i) t -> p c t i", i=4), km[0][:].rearrange("p t (c i) -> p c t i", i=4))
         km_c = sb.tile([P, I], U32, name="km_c", align_bytes=64)
         km_s = sb.tile([P, I], U8, name="km_s", align_bytes=64)
-        nc.vector.quantize_mx(out=km_c[:].bitcast(FP8X4), scales=km_s[:], in_=km_bf[:].rearrange("p i t -> p (i t)"))
+        for u in range(2):
+            cols = slice(u * 256, (u + 1) * 256)
+            dst = km_bf[:, cols, 2:4].rearrange("p (c i) t -> p c t i", i=4)
+            src = km[1][:, :, cols].rearrange("p t (c i) -> p c t i", i=4)
+            if u == 0:
+                nc.scalar.copy(dst, src)
+            else:
+                nc.vector.tensor_copy(dst, src)
+        for u in range(2):
+            cols = slice(u * 256, (u + 1) * 256)
+            nc.vector.quantize_mx(out=km_c[:, cols].bitcast(FP8X4), scales=km_s[:, cols], in_=km_bf[:, cols, :].rearrange("p i t -> p (i t)"))
 
         q_bf = sb.tile([P, PACK, P, PACK], BF16, name="q_bf", align_bytes=64)
-        for h in range(4):
-            dst = q_bf[:, :, h * 32 : (h + 1) * 32, :].rearrange("p t m j -> p m j t")
-            src = q_raw[h][:].rearrange("p j (m t) -> p m j t", t=PACK)
-            nc.scalar.copy(dst, src)
+        for lo, hi in ((0, 84), (84, 128)):
+            dst = q_bf[:, :, lo:hi, :].rearrange("p t m j -> p m j t")
+            src = q_raw[:, :, 4 * lo : 4 * hi].rearrange("p j (m t) -> p m j t", t=PACK)
+            if lo:
+                nc.scalar.copy(dst, src)
+            else:
+                nc.vector.tensor_copy(dst, src)
 
         y = sb.tile([P, PACK, I], F32, name="y")
         out_rows = out_0.rearrange("(p t) i -> p t i", t=PACK)
@@ -131,7 +138,12 @@ def tile_attend_lowrankdelta_pl_kernel(tc, query, up, lat_words, lat_scales, key
             e, s = probs[t]
             r = sb.tile([P, 1], F32, name=f"r{t}")
             nc.vector.reciprocal(r[:], s[:])
-            nc.vector.tensor_scalar(y[:, t, :], e[:], r[:], 512.0, ALU.mult, ALU.mult)
+            if t == 2:
+                r2 = sb.tile([P, 1], F32, name="r2x")
+                nc.vector.tensor_scalar(r2[:], r[:], 512.0, None, ALU.mult)
+                nc.scalar.activation(y[:, t, :], e[:], ACT.Copy, scale=r2[:])
+            else:
+                nc.vector.tensor_scalar(y[:, t, :], e[:], r[:], 512.0, ALU.mult, ALU.mult)
             nc.sync.dma_start(out_rows[:, t, :], y[:, t, :])
 
         y_bf = sb.tile([P, I, PACK], BF16, name="y_bf", align_bytes=64)

@@ -65,8 +65,8 @@ def tile_attend_lowrankdelta_pl_kernel(tc, query, up, lat_words, lat_scales, key
 
         up_bf = sb.tile([P, PACK, P, PACK], BF16, name="up_bf", align_bytes=64)
         for h in range(2):
-            dst = up_bf[:, :, h * 64 : (h + 1) * 64, :].rearrange("p t m j -> p m j t")
-            src = up_raw[:, :, h * 256 : (h + 1) * 256].rearrange("p j (m t) -> p m j t", t=PACK)
+            dst = up_bf[:, :, h * 64 : (h + 1) * 64, :].rearrange("p (u v) m j -> p u m j v", v=2)
+            src = up_raw[:, :, h * 256 : (h + 1) * 256].rearrange("p j (m u v) -> p u m j v", u=2, v=2)
             if h == 0:
                 nc.scalar.copy(dst, src)
             else:
@@ -107,10 +107,10 @@ def tile_attend_lowrankdelta_pl_kernel(tc, query, up, lat_words, lat_scales, key
             nc.vector.quantize_mx(out=km_c[:, cols].bitcast(FP8X4), scales=km_s[:, cols], in_=km_bf[:, cols, :].rearrange("p i t -> p (i t)"))
 
         q_bf = sb.tile([P, PACK, P, PACK], BF16, name="q_bf", align_bytes=64)
-        for lo, hi in ((0, 84), (84, 128)):
-            dst = q_bf[:, :, lo:hi, :].rearrange("p t m j -> p m j t")
-            src = q_raw[:, :, 4 * lo : 4 * hi].rearrange("p j (m t) -> p m j t", t=PACK)
-            if lo:
+        for u in range(2):
+            dst = q_bf[:, 2 * u : 2 * u + 2, :, :].rearrange("p v m j -> p m j v")
+            src = q_raw[:].rearrange("p j (m t) -> p m j t", t=PACK)[:, :, :, 2 * u : 2 * u + 2]
+            if u:
                 nc.scalar.copy(dst, src)
             else:
                 nc.vector.tensor_copy(dst, src)
@@ -126,7 +126,18 @@ def tile_attend_lowrankdelta_pl_kernel(tc, query, up, lat_words, lat_scales, key
             nc.tensor.matmul_mx(out=a[:], lhsT=q_c[:].bitcast(FP8X4), lhsT_scale=q_s[:],
                                 rhs=km_c[:].bitcast(FP8X4), rhs_scale=km_s[:], start=True, stop=True)
             scores.append(a)
-        probs = []
+        probs, recips = [], []
+
+        def invert(t):
+            r = sb.tile([P, 1], F32, name=f"r{t}")
+            nc.vector.reciprocal(r[:], probs[t][1][:])
+            recips.append(r)
+
+        def scale(t):
+            nc.vector.tensor_scalar(y[:, t, :], probs[t][0][:], recips[t][:], 512.0, ALU.mult, ALU.mult)
+            nc.sync.dma_start(out_rows[:, t, :], y[:, t, :])
+
+        r0x = sb.tile([P, 1], F32, name="r0x")
         for t in range(PACK):
             nmax = sb.tile([P, 1], F32, name=f"nmax{t}")
             nc.vector.tensor_reduce(nmax[:], scores[t][:], AX.X, ALU.max, negate=True)
@@ -134,17 +145,16 @@ def tile_attend_lowrankdelta_pl_kernel(tc, query, up, lat_words, lat_scales, key
             s = sb.tile([P, 1], F32, name=f"s{t}")
             nc.scalar.activation(e[:], scores[t][:], ACT.Exp, bias=nmax[:], scale=1.0, accum_out=s[:])
             probs.append((e, s))
-        for t in range(PACK):
-            e, s = probs[t]
-            r = sb.tile([P, 1], F32, name=f"r{t}")
-            nc.vector.reciprocal(r[:], s[:])
+            if t >= 1:
+                invert(t - 1)
             if t == 2:
-                r2 = sb.tile([P, 1], F32, name="r2x")
-                nc.vector.tensor_scalar(r2[:], r[:], 512.0, None, ALU.mult)
-                nc.scalar.activation(y[:, t, :], e[:], ACT.Copy, scale=r2[:])
-            else:
-                nc.vector.tensor_scalar(y[:, t, :], e[:], r[:], 512.0, ALU.mult, ALU.mult)
-            nc.sync.dma_start(out_rows[:, t, :], y[:, t, :])
+                nc.vector.tensor_scalar(r0x[:], recips[0][:], 512.0, None, ALU.mult)
+        scale(1)
+        scale(2)
+        invert(3)
+        nc.scalar.activation(y[:, 0, :], probs[0][0][:], ACT.Copy, scale=r0x[:])
+        nc.sync.dma_start(out_rows[:, 0, :], y[:, 0, :])
+        scale(3)
 
         y_bf = sb.tile([P, I, PACK], BF16, name="y_bf", align_bytes=64)
         for lo, hi, eng in ((0, 256, 0), (384, 512, 1), (256, 384, 0)):

@@ -30,22 +30,17 @@ def tile_attend_lowrankdelta_pl_kernel(tc, query, up, lat_words, lat_scales, key
         offsets = sb.tile([P, I // 16], U16, name="offsets")
         nc.sync.dma_start(offsets[:], offs)
 
-        lat_s = sb.tile([P, T], U8, name="lat_s", align_bytes=64)
-        nc.vector.memset(lat_s[:].bitcast(I32), 0)
-        warm_in = sb.tile([P, 1], F32, name="warm_in")
-        warm_out = sb.tile([P, 1], F32, name="warm_out")
-        nc.vector.memset(warm_in[:], 0.0)
-        for g in range(4):
-            nc.scalar.dma_start(lat_s[32 * g : 32 * g + 4, :].bitcast(I32), lat_scales[0, 4 * g : 4 * g + 4, :].bitcast(I32))
-        nc.scalar.activation(warm_out[:], warm_in[:], ACT.Exp)
-
         lat_w = sb.tile([P, T], U16, name="lat_w", align_bytes=64)
         nc.sync.dma_start(lat_w[:].bitcast(I32), lat_words[0].bitcast(I32))
 
-        up_rows = up.rearrange("(p j) c -> p j c", j=PACK)
+        lat_s = sb.tile([P, T], U8, name="lat_s", align_bytes=64)
+        nc.vector.memset(lat_s[:, : T // 2].bitcast(I32), 0)
+        nc.gpsimd.memset(lat_s[:, T // 2 :].bitcast(I32), 0)
+        for g in range(4):
+            nc.sync.dma_start(lat_s[g:P:32, :].bitcast(I32), lat_scales[0, g:16:4, :].bitcast(I32))
+
         up_raw = sb.tile([P, PACK, D], F32, name="up_raw")
-        for h in range(2):
-            nc.sync.dma_start(up_raw[:, 2 * h : 2 * h + 2, :], up_rows[:, 2 * h : 2 * h + 2, :])
+        nc.sync.dma_start(up_raw[:], up.rearrange("(p j) c -> p j c", j=PACK))
 
         key_rows = keys.rearrange("(p j) c -> p j c", j=PACK)
         key_pl = []
@@ -55,25 +50,30 @@ def tile_attend_lowrankdelta_pl_kernel(tc, query, up, lat_words, lat_scales, key
             key_pl.append(pl)
 
         q_rows = query.rearrange("(p j) c -> p j c", j=PACK)
-        q_raw = sb.tile([P, PACK, Q], F32, name="q_raw")
-        nc.sync.dma_start(q_raw[:], q_rows)
+        q_raw = []
+        for h in range(2):
+            raw = sb.tile([P, PACK, Q // 2], F32, name=f"q_raw{h}")
+            nc.sync.dma_start(raw[:], q_rows[:, :, h * 256 : (h + 1) * 256])
+            q_raw.append(raw)
 
-        g_s = sb.tile([P, I], U8, name="g_s", align_bytes=64)
-        nc.vector.tensor_copy(g_s[:], lat_s[:].indirect(offsets[:]))
         g_w = sb.tile([P, I], U16, name="g_w", align_bytes=64)
         nc.vector.tensor_copy(g_w[:], lat_w[:].indirect(offsets[:]))
+        g_s = sb.tile([P, I], U8, name="g_s", align_bytes=64)
+        nc.vector.tensor_copy(g_s[:], lat_s[:].indirect(offsets[:]))
 
         up_bf = sb.tile([P, PACK, P, PACK], BF16, name="up_bf", align_bytes=64)
-        for h in range(2):
-            dst = up_bf[:, :, h * 64 : (h + 1) * 64, :].rearrange("p (u v) m j -> p u m j v", v=2)
-            src = up_raw[:, :, h * 256 : (h + 1) * 256].rearrange("p j (m u v) -> p u m j v", u=2, v=2)
-            if h == 0:
+        up_c = sb.tile([P, D], U32, name="up_c", align_bytes=64)
+        up_s = sb.tile([P, D], U8, name="up_s", align_bytes=64)
+        for u in range(2):
+            dst = up_bf[:, 2 * u : 2 * u + 2, :, :].rearrange("p v m j -> p m j v")
+            src = up_raw[:].rearrange("p j (m t) -> p m j t", t=PACK)[:, :, :, 2 * u : 2 * u + 2]
+            if u:
                 nc.scalar.copy(dst, src)
             else:
                 nc.vector.tensor_copy(dst, src)
-        up_c = sb.tile([P, D], U32, name="up_c", align_bytes=64)
-        up_s = sb.tile([P, D], U8, name="up_s", align_bytes=64)
-        nc.vector.quantize_mx(out=up_c[:].bitcast(FP8X4), scales=up_s[:], in_=up_bf[:].rearrange("p t m j -> p (t m j)"))
+            cols = slice(u * 256, (u + 1) * 256)
+            nc.vector.quantize_mx(out=up_c[:, cols].bitcast(FP8X4), scales=up_s[:, cols],
+                                  in_=up_bf[:, 2 * u : 2 * u + 2, :, :].rearrange("p v m j -> p (v m j)"))
 
         km_bf = sb.tile([P, I, PACK], BF16, name="km_bf", align_bytes=64)
         km = [sb.tile([P, 2, I], F32, name=f"km{h}") for h in range(2)]
@@ -107,10 +107,10 @@ def tile_attend_lowrankdelta_pl_kernel(tc, query, up, lat_words, lat_scales, key
             nc.vector.quantize_mx(out=km_c[:, cols].bitcast(FP8X4), scales=km_s[:, cols], in_=km_bf[:, cols, :].rearrange("p i t -> p (i t)"))
 
         q_bf = sb.tile([P, PACK, P, PACK], BF16, name="q_bf", align_bytes=64)
-        for u in range(2):
-            dst = q_bf[:, 2 * u : 2 * u + 2, :, :].rearrange("p v m j -> p m j v")
-            src = q_raw[:].rearrange("p j (m t) -> p m j t", t=PACK)[:, :, :, 2 * u : 2 * u + 2]
-            if u:
+        for h, u in ((0, 0), (0, 1), (1, 0), (1, 1)):
+            dst = q_bf[:, 2 * u : 2 * u + 2, h * 64 : (h + 1) * 64, :].rearrange("p v m j -> p m j v")
+            src = q_raw[h][:].rearrange("p j (m t) -> p m j t", t=PACK)[:, :, :, 2 * u : 2 * u + 2]
+            if (h, u) != (1, 0):
                 nc.scalar.copy(dst, src)
             else:
                 nc.vector.tensor_copy(dst, src)
@@ -135,7 +135,6 @@ def tile_attend_lowrankdelta_pl_kernel(tc, query, up, lat_words, lat_scales, key
 
         def scale(t):
             nc.vector.tensor_scalar(y[:, t, :], probs[t][0][:], recips[t][:], 512.0, ALU.mult, ALU.mult)
-            nc.sync.dma_start(out_rows[:, t, :], y[:, t, :])
 
         r0x = sb.tile([P, 1], F32, name="r0x")
         for t in range(PACK):
@@ -149,12 +148,13 @@ def tile_attend_lowrankdelta_pl_kernel(tc, query, up, lat_words, lat_scales, key
                 invert(t - 1)
             if t == 2:
                 nc.vector.tensor_scalar(r0x[:], recips[0][:], 512.0, None, ALU.mult)
-        scale(1)
-        scale(2)
+        for t in (1, 2):
+            scale(t)
+            nc.sync.dma_start(out_rows[:, t, :], y[:, t, :])
         invert(3)
         nc.scalar.activation(y[:, 0, :], probs[0][0][:], ACT.Copy, scale=r0x[:])
-        nc.sync.dma_start(out_rows[:, 0, :], y[:, 0, :])
         scale(3)
+        nc.sync.dma_start(out_rows[:, 0:4:3, :], y[:, 0:4:3, :])
 
         y_bf = sb.tile([P, I, PACK], BF16, name="y_bf", align_bytes=64)
         for lo, hi, eng in ((0, 256, 0), (384, 512, 1), (256, 384, 0)):
@@ -174,4 +174,4 @@ def tile_attend_lowrankdelta_pl_kernel(tc, query, up, lat_words, lat_scales, key
             nc.sync.dma_start(words[:, cols], y_c[:, cols].bitcast(I32))
         for g in range(4):
             eng = nc.scalar if g % 2 else nc.sync
-            eng.dma_start(out_2[0, 4 * g : 4 * g + 4, :].bitcast(I32), y_s[32 * g : 32 * g + 4, :].bitcast(I32))
+            eng.dma_start(out_2[0, g:16:4, :].bitcast(I32), y_s[g:P:32, :].bitcast(I32))

@@ -28,10 +28,10 @@ def tile_attend_lowrankdelta_pl_kernel(tc, query, up, lat_words, lat_scales, key
         ps = ctx.enter_context(tc.psum_pool(name="ps", bufs=1))
 
         offsets = sb.tile([P, I // 16], U16, name="offsets")
-        nc.sync.dma_start(offsets[:], offs)
 
         lat_w = sb.tile([P, T], U16, name="lat_w", align_bytes=64)
         nc.sync.dma_start(lat_w[:].bitcast(I32), lat_words[0].bitcast(I32))
+        nc.sync.dma_start(offsets[:], offs)
 
         lat_s = sb.tile([P, T], U8, name="lat_s", align_bytes=64)
         nc.vector.memset(lat_s[:, : T // 2].bitcast(I32), 0)
@@ -157,7 +157,7 @@ def tile_attend_lowrankdelta_pl_kernel(tc, query, up, lat_words, lat_scales, key
         nc.sync.dma_start(out_rows[:, 0:4:3, :], y[:, 0:4:3, :])
 
         y_bf = sb.tile([P, I, PACK], BF16, name="y_bf", align_bytes=64)
-        for lo, hi, eng in ((0, 256, 0), (384, 512, 1), (256, 384, 0)):
+        for lo, hi, eng in ((0, 256, 0), (352, 512, 1), (256, 352, 0)):
             dst = y_bf[:, lo:hi, :].rearrange("p (c i) t -> p c t i", i=4)
             src = y[:, :, lo:hi].rearrange("p t (c i) -> p c t i", i=4)
             if eng:

from contextlib import ExitStack

import concourse.mybir as mybir

D, R, T, I, Q = 512, 512, 2048, 512, 512
FLOPS = 2 * R * D * I + 2 * D * Q * I

F32 = mybir.dt.float32
BF16 = mybir.dt.bfloat16
I32 = mybir.dt.int32
U32 = mybir.dt.uint32
U16 = mybir.dt.uint16
U8 = mybir.dt.uint8
FP8X4 = mybir.dt.float8_e4m3fn_x4
FP4X4 = mybir.dt.float4_e2m1fn_x4
ALU = mybir.AluOpType
ACT = mybir.ActivationFunctionType
AX = mybir.AxisListType

P = 128
PACK = 4


def tile_attend_lowrankdelta_pl_kernel(tc, query, up, lat_words, lat_scales, keys, offs, out_0, out_1, out_2):
    nc = tc.nc
    with ExitStack() as ctx:
        sb = ctx.enter_context(tc.tile_pool(name="sb", bufs=1))
        ps = ctx.enter_context(tc.psum_pool(name="ps", bufs=1))

        offsets = sb.tile([P, I // 16], U16, name="offsets")

        lat_w = sb.tile([P, T], U16, name="lat_w", align_bytes=64)
        nc.sync.dma_start(lat_w[:].bitcast(I32), lat_words[0].bitcast(I32))
        nc.sync.dma_start(offsets[:], offs)

        lat_s = sb.tile([P, T], U8, name="lat_s", align_bytes=64)
        nc.vector.memset(lat_s[:, : T // 2].bitcast(I32), 0)
        nc.gpsimd.memset(lat_s[:, T // 2 :].bitcast(I32), 0)
        for g in range(4):
            nc.sync.dma_start(lat_s[g:P:32, :].bitcast(I32), lat_scales[0, g:16:4, :].bitcast(I32))

        up_raw = sb.tile([P, PACK, D], F32, name="up_raw")
        nc.sync.dma_start(up_raw[:], up.rearrange("(p j) c -> p j c", j=PACK))

        key_rows = keys.rearrange("(p j) c -> p j c", j=PACK)
        key_pl = []
        for j in range(PACK):
            pl = sb.tile([P, T], F32, name=f"keys{j}")
            nc.sync.dma_start(pl[:], key_rows[:, j, :])
            key_pl.append(pl)

        q_rows = query.rearrange("(p j) c -> p j c", j=PACK)
        q_raw = []
        for h in range(2):
            raw = sb.tile([P, PACK, Q // 2], F32, name=f"q_raw{h}")
            nc.sync.dma_start(raw[:], q_rows[:, :, h * 256 : (h + 1) * 256])
            q_raw.append(raw)

        g_w = sb.tile([P, I], U16, name="g_w", align_bytes=64)
        nc.vector.tensor_copy(g_w[:], lat_w[:].indirect(offsets[:]))
        g_s = sb.tile([P, I], U8, name="g_s", align_bytes=64)
        nc.vector.tensor_copy(g_s[:], lat_s[:].indirect(offsets[:]))

        up_bf = sb.tile([P, PACK, P, PACK], BF16, name="up_bf", align_bytes=64)
        up_c = sb.tile([P, D], U32, name="up_c", align_bytes=64)
        up_s = sb.tile([P, D], U8, name="up_s", align_bytes=64)
        for u in range(2):
            dst = up_bf[:, 2 * u : 2 * u + 2, :, :].rearrange("p v m j -> p m j v")
            src = up_raw[:].rearrange("p j (m t) -> p m j t", t=PACK)[:, :, :, 2 * u : 2 * u + 2]
            if u:
                nc.scalar.copy(dst, src)
            else:
                nc.vector.tensor_copy(dst, src)
            cols = slice(u * 256, (u + 1) * 256)
            nc.vector.quantize_mx(out=up_c[:, cols].bitcast(FP8X4), scales=up_s[:, cols],
                                  in_=up_bf[:, 2 * u : 2 * u + 2, :, :].rearrange("p v m j -> p (v m j)"))

        km_bf = sb.tile([P, I, PACK], BF16, name="km_bf", align_bytes=64)
        km = [sb.tile([P, 2, I], F32, name=f"km{h}") for h in range(2)]
        for t in range(PACK):
            z = ps.tile([P, I], F32, name=f"z{t}")
            cols = slice(t * P, (t + 1) * P)
            nc.tensor.matmul_mx(out=z[:], lhsT=up_c[:, cols].bitcast(FP8X4), lhsT_scale=up_s[:, cols],
                                rhs=g_w[:].bitcast(FP4X4), rhs_scale=g_s[:], start=True, stop=True)
            z_sb = sb.tile([P, I], F32, name=f"z_sb{t}")
            nc.scalar.copy(z_sb[:], z[:])
            if t < PACK - 1:
                nc.vector.tensor_tensor(km[t // 2][:, t % 2, :], key_pl[t][:].indirect(offsets[:]), z_sb[:], ALU.add)
            else:
                for u in range(2):
                    nc.vector.tensor_tensor(km[1][:, 1, u * 256 : (u + 1) * 256], key_pl[t][:].indirect(offsets[:, u * 16 : (u + 1) * 16]),
                                            z_sb[:, u * 256 : (u + 1) * 256], ALU.add)
            if t == 1:
                nc.scalar.copy(km_bf[:, :, 0:2].rearrange("p (c i) t -> p c t i", i=4), km[0][:].rearrange("p t (c i) -> p c t i", i=4))
        km_c = sb.tile([P, I], U32, name="km_c", align_bytes=64)
        km_s = sb.tile([P, I], U8, name="km_s", align_bytes=64)
        for u in range(2):
            cols = slice(u * 256, (u + 1) * 256)
            dst = km_bf[:, cols, 2:4].rearrange("p (c i) t -> p c t i", i=4)
            src = km[1][:, :, cols].rearrange("p t (c i) -> p c t i", i=4)
            if u == 0:
                nc.scalar.copy(dst, src)
            else:
                nc.vector.tensor_copy(dst, src)
        for u in range(2):
            cols = slice(u * 256, (u + 1) * 256)
            nc.vector.quantize_mx(out=km_c[:, cols].bitcast(FP8X4), scales=km_s[:, cols], in_=km_bf[:, cols, :].rearrange("p i t -> p (i t)"))

        q_bf = sb.tile([P, PACK, P, PACK], BF16, name="q_bf", align_bytes=64)
        for h, u in ((0, 0), (0, 1), (1, 0), (1, 1)):
            dst = q_bf[:, 2 * u : 2 * u + 2, h * 64 : (h + 1) * 64, :].rearrange("p v m j -> p m j v")
            src = q_raw[h][:].rearrange("p j (m t) -> p m j t", t=PACK)[:, :, :, 2 * u : 2 * u + 2]
            if (h, u) != (1, 0):
                nc.scalar.copy(dst, src)
            else:
                nc.vector.tensor_copy(dst, src)

        y = sb.tile([P, PACK, I], F32, name="y")
        out_rows = out_0.rearrange("(p t) i -> p t i", t=PACK)
        scores = []
        for t in range(PACK):
            q_c = sb.tile([P, P], U32, name=f"q_c{t}", align_bytes=64)
            q_s = sb.tile([P, P], U8, name=f"q_s{t}", align_bytes=64)
            nc.vector.quantize_mx(out=q_c[:].bitcast(FP8X4), scales=q_s[:], in_=q_bf[:, t, :, :].rearrange("p m j -> p (m j)"))
            a = ps.tile([P, I], F32, name=f"a{t}")
            nc.tensor.matmul_mx(out=a[:], lhsT=q_c[:].bitcast(FP8X4), lhsT_scale=q_s[:],
                                rhs=km_c[:].bitcast(FP8X4), rhs_scale=km_s[:], start=True, stop=True)
            scores.append(a)
        probs, recips = [], []

        def invert(t):
            r = sb.tile([P, 1], F32, name=f"r{t}")
            nc.vector.reciprocal(r[:], probs[t][1][:])
            recips.append(r)

        def scale(t):
            nc.vector.tensor_scalar(y[:, t, :], probs[t][0][:], recips[t][:], 512.0, ALU.mult, ALU.mult)

        r0x = sb.tile([P, 1], F32, name="r0x")
        for t in range(PACK):
            nmax = sb.tile([P, 1], F32, name=f"nmax{t}")
            nc.vector.tensor_reduce(nmax[:], scores[t][:], AX.X, ALU.max, negate=True)
            e = sb.tile([P, I], F32, name=f"e{t}")
            s = sb.tile([P, 1], F32, name=f"s{t}")
            nc.scalar.activation(e[:], scores[t][:], ACT.Exp, bias=nmax[:], scale=1.0, accum_out=s[:])
            probs.append((e, s))
            if t >= 1:
                invert(t - 1)
            if t == 2:
                nc.vector.tensor_scalar(r0x[:], recips[0][:], 512.0, None, ALU.mult)
        for t in (1, 2):
            scale(t)
            nc.sync.dma_start(out_rows[:, t, :], y[:, t, :])
        invert(3)
        nc.scalar.activation(y[:, 0, :], probs[0][0][:], ACT.Copy, scale=r0x[:])
        scale(3)
        nc.sync.dma_start(out_rows[:, 0:4:3, :], y[:, 0:4:3, :])

        y_bf = sb.tile([P, I, PACK], BF16, name="y_bf", align_bytes=64)
        for lo, hi, eng in ((0, 256, 0), (352, 512, 1), (256, 352, 0)):
            dst = y_bf[:, lo:hi, :].rearrange("p (c i) t -> p c t i", i=4)
            src = y[:, :, lo:hi].rearrange("p t (c i) -> p c t i", i=4)
            if eng:
                nc.scalar.copy(dst, src)
            else:
                nc.vector.tensor_copy(dst, src)
        y_c = sb.tile([P, I], U32, name="y_c", align_bytes=64)
        y_s = sb.tile([P, I], U8, name="y_s", align_bytes=64)
        words = out_1[0].rearrange("p c t -> p (c t)").bitcast(I32)
        for h in range(2):
            cols = slice(h * 256, (h + 1) * 256)
            nc.vector.quantize_mx(out=y_c[:, cols].bitcast(FP8X4), scales=y_s[:, cols],
                                  in_=y_bf[:, cols, :].rearrange("p i t -> p (i t)"))
            nc.sync.dma_start(words[:, cols], y_c[:, cols].bitcast(I32))
        for g in range(4):
            eng = nc.scalar if g % 2 else nc.sync
            eng.dma_start(out_2[0, g:16:4, :].bitcast(I32), y_s[g:P:32, :].bitcast(I32))
